import numpy as np
import ml_dtypes


def mxq(x, axis, fmt="e4m3"):
    dtype, down = {"e4m3": (ml_dtypes.float8_e4m3fn, 7), "e5m2": (ml_dtypes.float8_e5m2, 14)}[fmt]
    v = np.moveaxis(np.asarray(x, np.float32).astype(ml_dtypes.bfloat16).astype(np.float64), axis, -1)
    blocks = v.reshape(v.shape[:-1] + (-1, 32))
    amax = np.abs(blocks).max(-1, keepdims=True)
    byte = np.maximum(np.where(amax > 0, np.frexp(amax)[1] - 1 + 127, 0) - down, 1)
    scale = np.exp2(byte - 127.0)
    codes = (blocks / scale).astype(np.float32).astype(dtype).astype(np.float64)
    return np.moveaxis((codes * scale).reshape(v.shape), -1, axis)


WIDE = False


def mx_kscale(k):
    if not WIDE:
        return np.ones(k)
    levels = np.array([10, -10, 5, -5, 0])
    if k % 512:
        return np.exp2(np.random.permutation(np.resize(levels, k // 32))).repeat(32)
    a = np.empty((k // 512, 16))
    for p in range(k // 512):
        a[p, :8] = np.random.permutation(np.resize(levels, 8))
        for g in range(8):
            far = levels[np.abs(levels - a[p, g]) >= 10]
            a[p, g + 8] = far[np.random.randint(len(far))]
    return np.exp2(a.ravel()).repeat(32)


def f64(x):
    return np.asarray(x).astype(np.float64)


def striped(idx):
    return np.tile(idx.reshape(-1, 16).T, (8, 1)).astype(np.uint16)


def unstriped(offs):
    return offs[:16].T.reshape(-1).astype(np.int64)


def relu(v):
    return np.maximum(v, 0.0)


K, T, S, N = 512, 2048, 1024, 128


def setup_inputs():
    n = np.random.standard_normal
    s = mx_kscale(K)[:, None]
    return {
        "xT": (n((K, S)) * s).astype(np.float32),
        "w": (n((K, N)) / np.sqrt(K) / s).astype(np.float32),
        "b": (0.3 * n((N, 1))).astype(np.float32),
        "gate": np.tile(np.random.uniform(0.2, 1.0, S), (N, 1)).astype(np.float32),
        "offs": striped(np.random.permutation(T)[:S]),
    }


def reference(xT, w, b, gate, offs):
    idx = unstriped(offs)
    xq = mxq(f64(xT), 0, "e4m3")
    y = mxq(f64(w), 0, "e4m3").T @ xq
    y = relu(y + f64(b))
    out = np.zeros((N, T))
    out[:, idx] = f64(gate) * y
    return out

@@ -1,0 +1,136 @@
+from contextlib import ExitStack
+
+import concourse.mybir as mybir
+
+K, T, S, N = 512, 2048, 1024, 128
+FLOPS = 2 * K * S * N
+
+F32 = mybir.dt.float32
+BF16 = mybir.dt.bfloat16
+U32 = mybir.dt.uint32
+U16 = mybir.dt.uint16
+U8 = mybir.dt.uint8
+FP8X4 = mybir.dt.float8_e4m3fn_x4
+RELU = mybir.ActivationFunctionType.Relu
+MULT = mybir.AluOpType.mult
+
+P = 128
+PACK = 4
+CHUNK = 256
+CHUNKS = S // CHUNK
+VECTOR_COLUMNS = (160, 256, 0, 0)
+
+
+def interleave(copy, grouped, raw, first, last):
+    copy(
+        out=grouped[:, first:last, :].rearrange("p (c i) j -> p c j i", i=4),
+        in_=raw[:, :, first:last].rearrange("p j (c i) -> p c j i", i=4),
+    )
+
+
+def tile_picked_place_lin_relu_sub_l_kernel(tc, xT, w, b, gate, offs, out):
+    nc = tc.nc
+    with ExitStack() as ctx:
+        held = ctx.enter_context(tc.tile_pool(name="held", bufs=1))
+        psum = ctx.enter_context(tc.psum_pool(name="psum", bufs=1))
+
+        offsets = held.tile([P, S // 16], U16, name="offsets")
+        window = held.tile([P, T], F32, name="window", align_bytes=64)
+        bias = held.tile([P, 1], F32, name="bias")
+        warm = held.tile([P, 1], F32, name="warm")
+        gates = held.tile([P, S], F32, name="gates", align_bytes=64)
+        w_raw = held.tile([P, PACK, N], F32, name="w_raw", align_bytes=64)
+        x_raw = [held.tile([P, PACK, CHUNK], F32, name=f"x_raw{c}", align_bytes=64) for c in range(CHUNKS)]
+
+        def load_x(c):
+            nc.sync.dma_start(
+                out=x_raw[c][:],
+                in_=xT[:, c * CHUNK : (c + 1) * CHUNK].rearrange("(p j) s -> p j s", j=PACK),
+            )
+
+        nc.sync.dma_start(out=w_raw[:], in_=w.rearrange("(p j) m -> p j m", j=PACK))
+        nc.scalar.dma_start(out=bias[:], in_=b)
+        load_x(0)
+        load_x(1)
+        nc.sync.dma_start(offsets[:], offs)
+        nc.sync.dma_start(out=gates[:, 0:CHUNK], in_=gate[:, 0:CHUNK])
+        load_x(2)
+        nc.sync.dma_start(out=gates[:, CHUNK:S], in_=gate[:, CHUNK:S])
+        load_x(3)
+
+        nc.vector.memset(warm[:], 0.0)
+        nc.scalar.activation(warm[:], warm[:], RELU)
+        nc.gpsimd.memset(window[:], 0.0)
+
+        w_grouped = held.tile([P, N, PACK], BF16, name="w_grouped", align_bytes=64)
+        w_codes = held.tile([P, N], U32, name="w_codes", align_bytes=64)
+        w_scales = held.tile([P, N], U8, name="w_scales", align_bytes=64)
+        interleave(nc.vector.tensor_copy, w_grouped, w_raw, 0, N)
+        nc.vector.quantize_mx(
+            out=w_codes[:].bitcast(FP8X4), scales=w_scales[:], in_=w_grouped[:].rearrange("p m j -> p (m j)")
+        )
+
+        x_grouped = [held.tile([P, CHUNK, PACK], BF16, name=f"x_grouped{c}", align_bytes=64) for c in range(CHUNKS)]
+        x_codes = [held.tile([P, CHUNK], U32, name=f"x_codes{c}", align_bytes=64) for c in range(CHUNKS)]
+        x_scales = [held.tile([P, CHUNK], U8, name=f"x_scales{c}", align_bytes=64) for c in range(CHUNKS)]
+        y = [held.tile([P, CHUNK], F32, name=f"y{c}", align_bytes=64) for c in range(CHUNKS)]
+        acc = [psum.tile([P, CHUNK], F32, name=f"acc{c}") for c in range(CHUNKS)]
+
+        def cast(c):
+            cut = VECTOR_COLUMNS[c]
+            if cut:
+                interleave(nc.vector.tensor_copy, x_grouped[c], x_raw[c], 0, cut)
+            if cut < CHUNK:
+                interleave(nc.scalar.copy, x_grouped[c], x_raw[c], cut, CHUNK)
+
+        def quantise(c):
+            nc.vector.quantize_mx(
+                out=x_codes[c][:].bitcast(FP8X4),
+                scales=x_scales[c][:],
+                in_=x_grouped[c][:].rearrange("p s j -> p (s j)"),
+            )
+
+        def multiply(c):
+            nc.tensor.matmul_mx(
+                out=acc[c][:],
+                lhsT=w_codes[:].bitcast(FP8X4),
+                lhsT_scale=w_scales[:],
+                rhs=x_codes[c][:].bitcast(FP8X4),
+                rhs_scale=x_scales[c][:],
+                start=True,
+                stop=True,
+            )
+
+        def rectify(c):
+            nc.scalar.activation(y[c][:], acc[c][:], RELU, bias=bias[:])
+
+        def scatter(c):
+            nc.vector.tensor_tensor(
+                window[:].indirect(offsets[:, c * CHUNK // 16 : (c + 1) * CHUNK // 16]),
+                y[c][:],
+                gates[:, c * CHUNK : (c + 1) * CHUNK],
+                MULT,
+            )
+
+        cast(0)
+        quantise(0)
+        multiply(0)
+        cast(1)
+        rectify(0)
+        quantise(1)
+        multiply(1)
+        scatter(0)
+        cast(2)
+        rectify(1)
+        quantise(2)
+        multiply(2)
+        scatter(1)
+        cast(3)
+        rectify(2)
+        quantise(3)
+        multiply(3)
+        scatter(2)
+        rectify(3)
+        scatter(3)
+
+        nc.sync.dma_start(out=out, in_=window[:])

@@ -18,7 +18,7 @@ P = 128
 PACK = 4
 CHUNK = 256
 CHUNKS = S // CHUNK
-VECTOR_COLUMNS = (160, 256, 0, 0)
+VECTOR_COLUMNS = (160, 160, 160, 0)
 
 
 def interleave(copy, grouped, raw, first, last):
@@ -38,7 +38,8 @@ def tile_picked_place_lin_relu_sub_l_kernel(tc, xT, w, b, gate, offs, out):
         window = held.tile([P, T], F32, name="window", align_bytes=64)
         bias = held.tile([P, 1], F32, name="bias")
         warm = held.tile([P, 1], F32, name="warm")
-        gates = held.tile([P, S], F32, name="gates", align_bytes=64)
+        gate_first = held.tile([P, CHUNK], F32, name="gate_first", align_bytes=64)
+        gate_rest = held.tile([P, S - CHUNK], F32, name="gate_rest", align_bytes=64)
         w_raw = held.tile([P, PACK, N], F32, name="w_raw", align_bytes=64)
         x_raw = [held.tile([P, PACK, CHUNK], F32, name=f"x_raw{c}", align_bytes=64) for c in range(CHUNKS)]
 
@@ -48,15 +49,15 @@ def tile_picked_place_lin_relu_sub_l_kernel(tc, xT, w, b, gate, offs, out):
                 in_=xT[:, c * CHUNK : (c + 1) * CHUNK].rearrange("(p j) s -> p j s", j=PACK),
             )
 
+        load_x(0)
         nc.sync.dma_start(out=w_raw[:], in_=w.rearrange("(p j) m -> p j m", j=PACK))
         nc.scalar.dma_start(out=bias[:], in_=b)
-        load_x(0)
         load_x(1)
-        nc.sync.dma_start(offsets[:], offs)
-        nc.sync.dma_start(out=gates[:, 0:CHUNK], in_=gate[:, 0:CHUNK])
         load_x(2)
-        nc.sync.dma_start(out=gates[:, CHUNK:S], in_=gate[:, CHUNK:S])
+        nc.sync.dma_start(offsets[:], offs)
+        nc.sync.dma_start(out=gate_first[:], in_=gate[:, 0:CHUNK])
         load_x(3)
+        nc.sync.dma_start(out=gate_rest[:], in_=gate[:, CHUNK:S])
 
         nc.vector.memset(warm[:], 0.0)
         nc.scalar.activation(warm[:], warm[:], RELU)
@@ -108,7 +109,7 @@ def tile_picked_place_lin_relu_sub_l_kernel(tc, xT, w, b, gate, offs, out):
             nc.vector.tensor_tensor(
                 window[:].indirect(offsets[:, c * CHUNK // 16 : (c + 1) * CHUNK // 16]),
                 y[c][:],
-                gates[:, c * CHUNK : (c + 1) * CHUNK],
+                gate_first[:] if c == 0 else gate_rest[:, (c - 1) * CHUNK : c * CHUNK],
                 MULT,
             )
 
@@ -119,18 +120,18 @@ def tile_picked_place_lin_relu_sub_l_kernel(tc, xT, w, b, gate, offs, out):
         rectify(0)
         quantise(1)
         multiply(1)
-        scatter(0)
         cast(2)
         rectify(1)
         quantise(2)
         multiply(2)
-        scatter(1)
-        cast(3)
         rectify(2)
+        cast(3)
         quantise(3)
         multiply(3)
-        scatter(2)
         rectify(3)
+        scatter(0)
+        scatter(1)
+        scatter(2)
         scatter(3)
 
         nc.sync.dma_start(out=out, in_=window[:])

@@ -18,7 +18,7 @@ P = 128
 PACK = 4
 CHUNK = 256
 CHUNKS = S // CHUNK
-VECTOR_COLUMNS = (160, 160, 160, 0)
+VECTOR_COLUMNS = (160, 192, 112, 0)
 
 
 def interleave(copy, grouped, raw, first, last):
@@ -53,9 +53,9 @@ def tile_picked_place_lin_relu_sub_l_kernel(tc, xT, w, b, gate, offs, out):
         nc.sync.dma_start(out=w_raw[:], in_=w.rearrange("(p j) m -> p j m", j=PACK))
         nc.scalar.dma_start(out=bias[:], in_=b)
         load_x(1)
-        load_x(2)
         nc.sync.dma_start(offsets[:], offs)
         nc.sync.dma_start(out=gate_first[:], in_=gate[:, 0:CHUNK])
+        load_x(2)
         load_x(3)
         nc.sync.dma_start(out=gate_rest[:], in_=gate[:, CHUNK:S])
 
@@ -117,21 +117,21 @@ def tile_picked_place_lin_relu_sub_l_kernel(tc, xT, w, b, gate, offs, out):
         quantise(0)
         multiply(0)
         cast(1)
-        rectify(0)
         quantise(1)
         multiply(1)
+        rectify(0)
         cast(2)
-        rectify(1)
         quantise(2)
         multiply(2)
-        rectify(2)
+        scatter(0)
+        rectify(1)
         cast(3)
         quantise(3)
         multiply(3)
-        rectify(3)
-        scatter(0)
         scatter(1)
+        rectify(2)
         scatter(2)
+        rectify(3)
         scatter(3)
 
         nc.sync.dma_start(out=out, in_=window[:])

@@ -38,8 +38,10 @@ def tile_picked_place_lin_relu_sub_l_kernel(tc, xT, w, b, gate, offs, out):
         window = held.tile([P, T], F32, name="window", align_bytes=64)
         bias = held.tile([P, 1], F32, name="bias")
         warm = held.tile([P, 1], F32, name="warm")
-        gate_first = held.tile([P, CHUNK], F32, name="gate_first", align_bytes=64)
-        gate_rest = held.tile([P, S - CHUNK], F32, name="gate_rest", align_bytes=64)
+        gate_0 = held.tile([P, CHUNK], F32, name="gate_0", align_bytes=64)
+        gate_1 = held.tile([P, CHUNK], F32, name="gate_1", align_bytes=64)
+        gate_23 = held.tile([P, 2 * CHUNK], F32, name="gate_23", align_bytes=64)
+        gates = (gate_0[:], gate_1[:], gate_23[:, 0:CHUNK], gate_23[:, CHUNK : 2 * CHUNK])
         w_raw = held.tile([P, PACK, N], F32, name="w_raw", align_bytes=64)
         x_raw = [held.tile([P, PACK, CHUNK], F32, name=f"x_raw{c}", align_bytes=64) for c in range(CHUNKS)]
 
@@ -54,10 +56,11 @@ def tile_picked_place_lin_relu_sub_l_kernel(tc, xT, w, b, gate, offs, out):
         nc.scalar.dma_start(out=bias[:], in_=b)
         load_x(1)
         nc.sync.dma_start(offsets[:], offs)
-        nc.sync.dma_start(out=gate_first[:], in_=gate[:, 0:CHUNK])
+        nc.sync.dma_start(out=gate_0[:], in_=gate[:, 0:CHUNK])
         load_x(2)
         load_x(3)
-        nc.sync.dma_start(out=gate_rest[:], in_=gate[:, CHUNK:S])
+        nc.sync.dma_start(out=gate_1[:], in_=gate[:, CHUNK : 2 * CHUNK])
+        nc.sync.dma_start(out=gate_23[:], in_=gate[:, 2 * CHUNK : S])
 
         nc.vector.memset(warm[:], 0.0)
         nc.scalar.activation(warm[:], warm[:], RELU)
@@ -109,7 +112,7 @@ def tile_picked_place_lin_relu_sub_l_kernel(tc, xT, w, b, gate, offs, out):
             nc.vector.tensor_tensor(
                 window[:].indirect(offsets[:, c * CHUNK // 16 : (c + 1) * CHUNK // 16]),
                 y[c][:],
-                gate_first[:] if c == 0 else gate_rest[:, (c - 1) * CHUNK : c * CHUNK],
+                gates[c],
                 MULT,
             )
 

from contextlib import ExitStack

import concourse.mybir as mybir

K, T, S, N = 512, 2048, 1024, 128
FLOPS = 2 * K * S * N

F32 = mybir.dt.float32
BF16 = mybir.dt.bfloat16
U32 = mybir.dt.uint32
U16 = mybir.dt.uint16
U8 = mybir.dt.uint8
FP8X4 = mybir.dt.float8_e4m3fn_x4
RELU = mybir.ActivationFunctionType.Relu
MULT = mybir.AluOpType.mult

P = 128
PACK = 4
CHUNK = 256
CHUNKS = S // CHUNK
VECTOR_COLUMNS = (160, 192, 112, 0)


def interleave(copy, grouped, raw, first, last):
    copy(
        out=grouped[:, first:last, :].rearrange("p (c i) j -> p c j i", i=4),
        in_=raw[:, :, first:last].rearrange("p j (c i) -> p c j i", i=4),
    )


def tile_picked_place_lin_relu_sub_l_kernel(tc, xT, w, b, gate, offs, out):
    nc = tc.nc
    with ExitStack() as ctx:
        held = ctx.enter_context(tc.tile_pool(name="held", bufs=1))
        psum = ctx.enter_context(tc.psum_pool(name="psum", bufs=1))

        offsets = held.tile([P, S // 16], U16, name="offsets")
        window = held.tile([P, T], F32, name="window", align_bytes=64)
        bias = held.tile([P, 1], F32, name="bias")
        warm = held.tile([P, 1], F32, name="warm")
        gate_0 = held.tile([P, CHUNK], F32, name="gate_0", align_bytes=64)
        gate_1 = held.tile([P, CHUNK], F32, name="gate_1", align_bytes=64)
        gate_23 = held.tile([P, 2 * CHUNK], F32, name="gate_23", align_bytes=64)
        gates = (gate_0[:], gate_1[:], gate_23[:, 0:CHUNK], gate_23[:, CHUNK : 2 * CHUNK])
        w_raw = held.tile([P, PACK, N], F32, name="w_raw", align_bytes=64)
        x_raw = [held.tile([P, PACK, CHUNK], F32, name=f"x_raw{c}", align_bytes=64) for c in range(CHUNKS)]

        def load_x(c):
            nc.sync.dma_start(
                out=x_raw[c][:],
                in_=xT[:, c * CHUNK : (c + 1) * CHUNK].rearrange("(p j) s -> p j s", j=PACK),
            )

        load_x(0)
        nc.sync.dma_start(out=w_raw[:], in_=w.rearrange("(p j) m -> p j m", j=PACK))
        nc.scalar.dma_start(out=bias[:], in_=b)
        load_x(1)
        nc.sync.dma_start(offsets[:], offs)
        nc.sync.dma_start(out=gate_0[:], in_=gate[:, 0:CHUNK])
        load_x(2)
        load_x(3)
        nc.sync.dma_start(out=gate_1[:], in_=gate[:, CHUNK : 2 * CHUNK])
        nc.sync.dma_start(out=gate_23[:], in_=gate[:, 2 * CHUNK : S])

        nc.vector.memset(warm[:], 0.0)
        nc.scalar.activation(warm[:], warm[:], RELU)
        nc.gpsimd.memset(window[:], 0.0)

        w_grouped = held.tile([P, N, PACK], BF16, name="w_grouped", align_bytes=64)
        w_codes = held.tile([P, N], U32, name="w_codes", align_bytes=64)
        w_scales = held.tile([P, N], U8, name="w_scales", align_bytes=64)
        interleave(nc.vector.tensor_copy, w_grouped, w_raw, 0, N)
        nc.vector.quantize_mx(
            out=w_codes[:].bitcast(FP8X4), scales=w_scales[:], in_=w_grouped[:].rearrange("p m j -> p (m j)")
        )

        x_grouped = [held.tile([P, CHUNK, PACK], BF16, name=f"x_grouped{c}", align_bytes=64) for c in range(CHUNKS)]
        x_codes = [held.tile([P, CHUNK], U32, name=f"x_codes{c}", align_bytes=64) for c in range(CHUNKS)]
        x_scales = [held.tile([P, CHUNK], U8, name=f"x_scales{c}", align_bytes=64) for c in range(CHUNKS)]
        y = [held.tile([P, CHUNK], F32, name=f"y{c}", align_bytes=64) for c in range(CHUNKS)]
        acc = [psum.tile([P, CHUNK], F32, name=f"acc{c}") for c in range(CHUNKS)]

        def cast(c):
            cut = VECTOR_COLUMNS[c]
            if cut:
                interleave(nc.vector.tensor_copy, x_grouped[c], x_raw[c], 0, cut)
            if cut < CHUNK:
                interleave(nc.scalar.copy, x_grouped[c], x_raw[c], cut, CHUNK)

        def quantise(c):
            nc.vector.quantize_mx(
                out=x_codes[c][:].bitcast(FP8X4),
                scales=x_scales[c][:],
                in_=x_grouped[c][:].rearrange("p s j -> p (s j)"),
            )

        def multiply(c):
            nc.tensor.matmul_mx(
                out=acc[c][:],
                lhsT=w_codes[:].bitcast(FP8X4),
                lhsT_scale=w_scales[:],
                rhs=x_codes[c][:].bitcast(FP8X4),
                rhs_scale=x_scales[c][:],
                start=True,
                stop=True,
            )

        def rectify(c):
            nc.scalar.activation(y[c][:], acc[c][:], RELU, bias=bias[:])

        def scatter(c):
            nc.vector.tensor_tensor(
                window[:].indirect(offsets[:, c * CHUNK // 16 : (c + 1) * CHUNK // 16]),
                y[c][:],
                gates[c],
                MULT,
            )

        cast(0)
        quantise(0)
        multiply(0)
        cast(1)
        quantise(1)
        multiply(1)
        rectify(0)
        cast(2)
        quantise(2)
        multiply(2)
        scatter(0)
        rectify(1)
        cast(3)
        quantise(3)
        multiply(3)
        scatter(1)
        rectify(2)
        scatter(2)
        rectify(3)
        scatter(3)

        nc.sync.dma_start(out=out, in_=window[:])
